import numpy as np
import ml_dtypes


def mxq(x, axis, fmt="e4m3"):
    dtype, down = {"e4m3": (ml_dtypes.float8_e4m3fn, 7), "e5m2": (ml_dtypes.float8_e5m2, 14)}[fmt]
    v = np.moveaxis(np.asarray(x, np.float32).astype(ml_dtypes.bfloat16).astype(np.float64), axis, -1)
    blocks = v.reshape(v.shape[:-1] + (-1, 32))
    amax = np.abs(blocks).max(-1, keepdims=True)
    byte = np.maximum(np.where(amax > 0, np.frexp(amax)[1] - 1 + 127, 0) - down, 1)
    scale = np.exp2(byte - 127.0)
    codes = (blocks / scale).astype(np.float32).astype(dtype).astype(np.float64)
    return np.moveaxis((codes * scale).reshape(v.shape), -1, axis)


WIDE = False


def mx_kscale(k):
    if not WIDE:
        return np.ones(k)
    levels = np.array([30, -30])
    if k % 512:
        return np.exp2(np.random.permutation(np.resize(levels, k // 32))).repeat(32)
    a = np.empty((k // 512, 16))
    for p in range(k // 512):
        a[p, :8] = np.random.permutation(np.resize(levels, 8))
        for g in range(8):
            far = levels[np.abs(levels - a[p, g]) >= 10]
            a[p, g + 8] = far[np.random.randint(len(far))]
    return np.exp2(a.ravel()).repeat(32)


def f64(x):
    return np.asarray(x).astype(np.float64)


def striped(idx):
    return np.tile(np.asarray(idx).reshape(-1, 16).T, (8, 1)).astype(np.uint16)


def unstriped(offs):
    return offs[:16].T.reshape(-1).astype(np.int64)


E2M1 = np.array([0.0, 0.5, 1.0, 1.5, 2.0, 3.0, 4.0, 6.0, -0.0, -0.5, -1.0, -1.5, -2.0, -3.0, -4.0, -6.0])


def pack_weight(w, fmt):
    k, n = w.shape
    w = f64(np.asarray(w, np.float32).astype(ml_dtypes.bfloat16)).reshape(k // 32, 32, n)
    amax = np.abs(w).max(1)
    if fmt in ("e4m3", "e5m2"):
        byte = np.frexp(amax)[1] - 1 + 127 - (7 if fmt == "e4m3" else 14)
    else:
        mant, ex = np.frexp(amax / 6.0)
        byte = np.where(mant > 0.5, ex, ex - 1) + 127
    byte = np.clip(np.where(amax > 0, byte, 1), 1, 254)
    scaled = (w * np.exp2(127.0 - byte)[:, None, :]).reshape(k, n).astype(np.float32)
    by_word = np.ascontiguousarray(scaled.reshape(k // 512, 128, 4, n).transpose(0, 1, 3, 2))
    if fmt in ("e4m3", "e5m2"):
        words = by_word.astype(ml_dtypes.float8_e4m3fn if fmt == "e4m3" else ml_dtypes.float8_e5m2).view(np.uint8)
    else:
        c = by_word.astype(ml_dtypes.float4_e2m1fn).view(np.uint8) & 0xF
        words = (c[..., 0::2] | (c[..., 1::2] << 4)).reshape(k // 512, 128, 2 * n)
    return np.ascontiguousarray(words), np.ascontiguousarray(byte.astype(np.uint8).reshape(k // 512, 16, n))


def unpack_weight(words, scales, fmt):
    g, _, n = scales.shape
    words = np.ascontiguousarray(words).reshape(g, 128, n, -1)
    if fmt in ("e4m3", "e5m2"):
        vals = words.view(ml_dtypes.float8_e4m3fn if fmt == "e4m3" else ml_dtypes.float8_e5m2).astype(np.float64)
    else:
        nib = np.empty((g, 128, n, 4), np.uint8)
        nib[..., 0::2] = words & 0xF
        nib[..., 1::2] = words >> 4
        vals = E2M1[nib]
    vals = vals * np.repeat(np.exp2(scales.astype(np.float64) - 127.0), 8, axis=1)[..., None]
    return vals.transpose(0, 1, 3, 2).reshape(g * 512, n)


K, T, Z, J, R, N, L, E = 512, 1024, 1024, 256, 512, 256, 512, 1024


def setup_inputs():
    n = np.random.standard_normal
    idx = np.random.permutation(T)[:J]
    idx2 = np.random.permutation(Z)[:J]
    idx3 = np.random.permutation(E)[:J]
    fk = mx_kscale(K)
    fr = mx_kscale(R)
    fl = mx_kscale(L)
    xtp = pack_weight(n((K, T)) / fk[:, None], "e4m3")
    xop = pack_weight(n((K, Z)) / fk[:, None], "e2m1")
    wp = pack_weight(n((K, R)) * 1 / np.sqrt(K) * fk[:, None] * fr, "e5m2")
    w2p = pack_weight(n((K, R)) * 1 / np.sqrt(K) * fk[:, None] * fr, "e5m2")
    wbp = pack_weight(n((R, N)) * 1 / np.sqrt(R) / fr[:, None], "e5m2")
    sxp = pack_weight(n((L, J)) / fl[:, None], "e2m1")
    wsp = pack_weight(n((L, N)) * 1 / np.sqrt(L) * fl[:, None], "e5m2")
    return {
        "xt_words": xtp[0],
        "xt_scales": xtp[1],
        "xo_words": xop[0],
        "xo_scales": xop[1],
        "w_words": wp[0],
        "w_scales": wp[1],
        "w2_words": w2p[0],
        "w2_scales": w2p[1],
        "wb_words": wbp[0],
        "wb_scales": wbp[1],
        "sx_words": sxp[0],
        "sx_scales": sxp[1],
        "ws_words": wsp[0],
        "ws_scales": wsp[1],
        "offs": striped(idx),
        "offs2": striped(idx2),
        "offs3": striped(idx3),
    }


def reference(xt_words, xt_scales, xo_words, xo_scales, w_words, w_scales, w2_words, w2_scales, wb_words, wb_scales, sx_words, sx_scales, ws_words, ws_scales, offs, offs2, offs3):
    idx = unstriped(offs)
    idx2 = unstriped(offs2)
    idx3 = unstriped(offs3)
    xtu = unpack_weight(xt_words, xt_scales, "e4m3")
    xou = unpack_weight(xo_words, xo_scales, "e2m1")
    wu = unpack_weight(w_words, w_scales, "e5m2")
    w2u = unpack_weight(w2_words, w2_scales, "e5m2")
    wbu = unpack_weight(wb_words, wb_scales, "e5m2")
    sxu = unpack_weight(sx_words, sx_scales, "e2m1")
    wsu = unpack_weight(ws_words, ws_scales, "e5m2")
    xtidxg = xtu[:, idx]
    xoidx2g = xou[:, idx2]
    a = wu.T @ xtidxg + w2u.T @ xoidx2g
    b = w2u.T @ xtidxg + wu.T @ xoidx2g
    hid = np.maximum(a, b)
    hidq = mxq(hid, 0, "e4m3")
    p = wbu.T @ hidq + wsu.T @ sxu
    y = np.zeros((N, E))
    y[:, idx3] = p
    return y

@@ -1,0 +1,204 @@
+from contextlib import ExitStack
+
+import concourse.mybir as mybir
+
+K, T, Z, J, R, N, L, E = 512, 1024, 1024, 256, 512, 256, 512, 1024
+FLOPS = 2 * J * (4 * K * R + R * N + L * N)
+
+F32 = mybir.dt.float32
+BF16 = mybir.dt.bfloat16
+I32 = mybir.dt.int32
+U32 = mybir.dt.uint32
+U16 = mybir.dt.uint16
+U8 = mybir.dt.uint8
+E4M3 = mybir.dt.float8_e4m3fn_x4
+E5M2 = mybir.dt.float8_e5m2_x4
+E2M1 = mybir.dt.float4_e2m1fn_x4
+MAX = mybir.AluOpType.max
+COPY = mybir.ActivationFunctionType.Copy
+
+P = 128
+PACK = 4
+ROWS = 16
+HALF = 128
+
+
+def tile_list_crossed_direct_skip_scattered_kernel(
+    tc, xt_words, xt_scales, xo_words, xo_scales, w_words, w_scales, w2_words, w2_scales,
+    wb_words, wb_scales, sx_words, sx_scales, ws_words, ws_scales, offs, offs2, offs3, out,
+):
+    nc = tc.nc
+    with ExitStack() as ctx:
+        lists = ctx.enter_context(tc.tile_pool(name="lists", bufs=1))
+        sb = ctx.enter_context(tc.tile_pool(name="sb", bufs=1))
+        shared = ctx.enter_context(tc.tile_pool(name="shared", bufs=1))
+        staging = ctx.enter_context(tc.tile_pool(name="staging", bufs=1))
+        psum = ctx.enter_context(tc.psum_pool(name="psum", bufs=1))
+
+        def tile(name, width, dtype):
+            return sb.tile([P, width], dtype, name=name, align_bytes=64)
+
+        def load_words(dst, words):
+            flat = words[0] if words.ndim == 3 else words[0].rearrange("p c t -> p (c t)")
+            nc.sync.dma_start(out=dst.bitcast(I32), in_=flat.bitcast(I32))
+
+        def load_rows(queue, dst, col, scales):
+            width = scales.shape[2]
+            queue.dma_start(out=dst[0:ROWS, col : col + width].bitcast(I32), in_=scales[0].bitcast(I32))
+
+        def deal_rows(planes):
+            for q in range(1, 4):
+                nc.sync.dma_start(
+                    out=planes[32 * q : 32 * q + 4, :].bitcast(I32), in_=planes[4 * q : 4 * q + 4, :].bitcast(I32)
+                )
+
+        idx = lists.tile([P, J // 16], U16, name="idx")
+        idx2 = lists.tile([P, J // 16], U16, name="idx2")
+        idx3 = lists.tile([P, J // 16], U16, name="idx3")
+
+        xt_rows = tile("xt_rows", T, U8)
+        xo_rows = tile("xo_rows", Z, U8)
+        w_rows = staging.tile([P, 2 * R], U8, name="w_rows", offset=0, align_bytes=64)
+        nc.gpsimd.memset(xt_rows[:].bitcast(I32), 0)
+        nc.vector.memset(xo_rows[:].bitcast(I32), 0)
+        nc.gpsimd.memset(w_rows[:].bitcast(I32), 0)
+
+        xt_all = sb.tile([P, T], U32, name="xt_all", tag="table", align_bytes=64)
+        xo_all = shared.tile([P, Z], U16, name="xo_all", offset=3 * E)
+        w_raw = tile("w_raw", R, U32)
+        w2_raw = tile("w2_raw", R, U32)
+
+        nc.sync.dma_start(idx[:], offs)
+        nc.sync.dma_start(idx2[:], offs2)
+        load_rows(nc.scalar, xt_rows, 0, xt_scales)
+        load_rows(nc.scalar, xo_rows, 0, xo_scales)
+        load_rows(nc.scalar, w_rows, 0, w_scales)
+        load_rows(nc.scalar, w_rows, R, w2_scales)
+        load_words(xt_all[:], xt_words)
+        load_words(w_raw[:], w_words)
+        load_words(w2_raw[:], w2_words)
+        load_words(xo_all[:], xo_words)
+        nc.sync.dma_start(idx3[:], offs3)
+
+        xt_picked_rows = tile("xt_picked_rows", J, U8)
+        xo_picked_rows = staging.tile([P, J], U8, name="xo_picked_rows", offset=2 * R, align_bytes=64)
+        planes1 = tile("planes1", 2 * J + 2 * R, U8)
+        nc.vector.tensor_copy(xt_picked_rows[:], xt_rows[:].indirect(idx[:]))
+        nc.vector.tensor_copy(xo_picked_rows[:], xo_rows[:].indirect(idx2[:]))
+        nc.gpsimd.tensor_copy(
+            planes1[:, 2 * J :].rearrange("p (i t m) -> p i t m", i=2, t=PACK),
+            w_rows[:].rearrange("p (i m t) -> p i t m", i=2, t=PACK),
+        )
+        nc.vector.tensor_copy(planes1[:, 0:J].bitcast(I32), xt_picked_rows[:].bitcast(I32))
+        nc.vector.tensor_copy(planes1[:, J : 2 * J].bitcast(I32), xo_picked_rows[:].bitcast(I32))
+        deal_rows(planes1)
+
+        planes2 = staging.tile([P, 2 * N + J], U8, name="planes2", offset=2 * R + J // 2 - (2 * N + J), align_bytes=64)
+        nc.gpsimd.memset(planes2[:].bitcast(I32), 0)
+        load_rows(nc.sync, planes2, 0, wb_scales)
+        load_rows(nc.sync, planes2, N, ws_scales)
+        load_rows(nc.sync, planes2, 2 * N, sx_scales)
+
+        xt = staging.tile([P, J], U32, name="xt", offset=2 * R + J // 2, align_bytes=64)
+        xo = tile("xo", J, U16)
+        nc.vector.tensor_copy(xt[:], xt_all[:].indirect(idx[:]))
+        nc.vector.tensor_copy(xo[:], xo_all[:].indirect(idx2[:]))
+
+        second = sb.tile([P, 8 * N + 2 * J], U8, name="second", tag="table", align_bytes=64)
+        wb = second[:, 0 : 4 * N].bitcast(U32)
+        ws = second[:, 4 * N : 8 * N].bitcast(U32)
+        sx = second[:, 8 * N :].bitcast(U16)
+        load_words(ws, ws_words)
+        load_words(sx, sx_words)
+        load_words(wb, wb_words)
+        deal_rows(planes2)
+        pages = [shared.tile([P, E], F32, name="page%d" % n, offset=4 * E * n) for n in range(2)]
+        for page in pages:
+            nc.vector.memset(page[:], 0.0)
+
+        w = tile("w", R, U32)
+        w2 = tile("w2", R, U32)
+        for dst, raw in ((w, w_raw), (w2, w2_raw)):
+            nc.scalar.copy(dst[:].rearrange("p (t m) -> p m t", t=PACK), raw[:].rearrange("p (m t) -> p m t", t=PACK))
+
+        w_plane, w2_plane = 2 * J, 2 * J + R
+
+        def passes(bank, h, weight, weight_plane, picked, picked_dtype, picked_plane, first):
+            j0 = h * HALF
+            for t in range(PACK):
+                cols = slice(t * P, (t + 1) * P)
+                nc.tensor.matmul_mx(
+                    out=bank[:, cols],
+                    lhsT=weight[:, cols].bitcast(E5M2),
+                    lhsT_scale=planes1[:, weight_plane + t * P : weight_plane + (t + 1) * P],
+                    rhs=picked[:, j0 : j0 + HALF].bitcast(picked_dtype),
+                    rhs_scale=planes1[:, picked_plane + j0 : picked_plane + j0 + HALF],
+                    start=first and t == 0, stop=(not first) and t == PACK - 1,
+                )
+
+        hid_codes, hid_planes = [], []
+        for h in range(2):
+            a_bank = psum.tile([P, PACK * HALF], F32, name="a%d" % h)
+            b_bank = psum.tile([P, PACK * HALF], F32, name="b%d" % h)
+            steps = [
+                (a_bank, h, w, w_plane, xt, E4M3, 0, True),
+                (b_bank, h, w2, w2_plane, xt, E4M3, 0, True),
+                (a_bank, h, w2, w2_plane, xo, E2M1, J, False),
+                (b_bank, h, w, w_plane, xo, E2M1, J, False),
+            ]
+            for i in ((0, 1, 2, 3) if h == 0 else (0, 2, 1, 3)):
+                passes(*steps[i])
+            a_sb = tile("a_sb%d" % h, PACK * HALF, F32)
+            nc.scalar.copy(
+                a_sb[:].rearrange("p (j t) -> p j t", t=PACK), a_bank[:].rearrange("p (t j) -> p j t", t=PACK)
+            )
+            hid = tile("hid%d" % h, PACK * HALF, BF16)
+            codes = tile("hid_codes%d" % h, HALF, U32)
+            plane = tile("hid_plane%d" % h, HALF, U8)
+            quarters = [slice(0, HALF // 2), slice(HALF // 2, HALF)]
+            for js in quarters:
+                nc.vector.tensor_tensor(
+                    hid[:].rearrange("p (j t) -> p j t", t=PACK)[:, js, :],
+                    a_sb[:].rearrange("p (j t) -> p j t", t=PACK)[:, js, :],
+                    b_bank[:].rearrange("p (t j) -> p j t", t=PACK)[:, js, :],
+                    MAX,
+                )
+            for js in quarters:
+                nc.vector.quantize_mx(
+                    out=codes[:, js].bitcast(E4M3), scales=plane[:, js], in_=hid[:, PACK * js.start : PACK * js.stop]
+                )
+            hid_codes.append(codes)
+            hid_planes.append(plane)
+
+        for h in range(2):
+            j0 = h * HALF
+            places = idx3[:, h * HALF // 16 : (h + 1) * HALF // 16]
+            for n in range(2):
+                cols = slice(n * P, (n + 1) * P)
+                p_bank = psum.tile([P, HALF], F32, name="p%d%d" % (h, n))
+                nc.tensor.matmul_mx(
+                    out=p_bank[:],
+                    lhsT=ws[:, cols].bitcast(E5M2),
+                    lhsT_scale=planes2[:, N + n * P : N + (n + 1) * P],
+                    rhs=sx[:, j0 : j0 + HALF].bitcast(E2M1),
+                    rhs_scale=planes2[:, 2 * N + j0 : 2 * N + j0 + HALF],
+                    start=True, stop=False,
+                )
+                nc.tensor.matmul_mx(
+                    out=p_bank[:],
+                    lhsT=wb[:, cols].bitcast(E5M2),
+                    lhsT_scale=planes2[:, cols],
+                    rhs=hid_codes[h][:].bitcast(E4M3),
+                    rhs_scale=hid_planes[h][:],
+                    start=False, stop=True,
+                )
+                p_sb = tile("p_sb%d%d" % (h, n), HALF, F32)
+                if (h, n) == (1, 0):
+                    nc.vector.tensor_copy(p_sb[:], p_bank[:])
+                    nc.vector.tensor_copy(pages[n][:].indirect(places), p_sb[:])
+                else:
+                    nc.scalar.copy(p_sb[:], p_bank[:])
+                    nc.scalar.activation(pages[n][:].indirect(places), p_sb[:], COPY)
+
+        for n in range(2):
+            nc.sync.dma_start(out=out[n * P : (n + 1) * P, :], in_=pages[n][:])

@@ -31,26 +31,23 @@ def tile_list_crossed_direct_skip_scattered_kernel(
     with ExitStack() as ctx:
         lists = ctx.enter_context(tc.tile_pool(name="lists", bufs=1))
         sb = ctx.enter_context(tc.tile_pool(name="sb", bufs=1))
-        shared = ctx.enter_context(tc.tile_pool(name="shared", bufs=1))
-        staging = ctx.enter_context(tc.tile_pool(name="staging", bufs=1))
         psum = ctx.enter_context(tc.psum_pool(name="psum", bufs=1))
 
-        def tile(name, width, dtype):
-            return sb.tile([P, width], dtype, name=name, align_bytes=64)
+        def tile(name, width, dtype, tag=None):
+            return sb.tile([P, width], dtype, name=name, tag=tag or name, align_bytes=64)
 
-        def load_words(dst, words):
+        def load_words(queue, dst, words):
             flat = words[0] if words.ndim == 3 else words[0].rearrange("p c t -> p (c t)")
-            nc.sync.dma_start(out=dst.bitcast(I32), in_=flat.bitcast(I32))
+            queue.dma_start(out=dst.bitcast(I32), in_=flat.bitcast(I32))
 
         def load_rows(queue, dst, col, scales):
             width = scales.shape[2]
-            queue.dma_start(out=dst[0:ROWS, col : col + width].bitcast(I32), in_=scales[0].bitcast(I32))
+            rows = scales[0].bitcast(I32).unsqueeze(1).to_broadcast([ROWS, P // ROWS, width // 4])
+            queue.dma_start(out=dst[:, col : col + width].bitcast(I32), in_=rows)
 
-        def deal_rows(planes):
-            for q in range(1, 4):
-                nc.sync.dma_start(
-                    out=planes[32 * q : 32 * q + 4, :].bitcast(I32), in_=planes[4 * q : 4 * q + 4, :].bitcast(I32)
-                )
+        def deal_rows(queue, rows):
+            for r in range(1, 4):
+                queue.dma_start(out=rows[r:P:32, :].bitcast(I32), in_=rows[8 * r : P : 32, :].bitcast(I32))
 
         idx = lists.tile([P, J // 16], U16, name="idx")
         idx2 = lists.tile([P, J // 16], U16, name="idx2")
@@ -58,101 +55,97 @@ def tile_list_crossed_direct_skip_scattered_kernel(
 
         xt_rows = tile("xt_rows", T, U8)
         xo_rows = tile("xo_rows", Z, U8)
-        w_rows = staging.tile([P, 2 * R], U8, name="w_rows", offset=0, align_bytes=64)
-        nc.gpsimd.memset(xt_rows[:].bitcast(I32), 0)
-        nc.vector.memset(xo_rows[:].bitcast(I32), 0)
-        nc.gpsimd.memset(w_rows[:].bitcast(I32), 0)
-
-        xt_all = sb.tile([P, T], U32, name="xt_all", tag="table", align_bytes=64)
-        xo_all = shared.tile([P, Z], U16, name="xo_all", offset=3 * E)
+        xo_all = tile("xo_all", Z, U16)
+        w_rows = tile("w_rows", R, U8)
+        w2_rows = tile("w2_rows", R, U8)
+        xt_all = tile("xt_all", T, U32, tag="table")
         w_raw = tile("w_raw", R, U32)
         w2_raw = tile("w2_raw", R, U32)
 
         nc.sync.dma_start(idx[:], offs)
-        nc.sync.dma_start(idx2[:], offs2)
         load_rows(nc.scalar, xt_rows, 0, xt_scales)
+        load_rows(nc.sync, w_rows, 0, w_scales)
+        load_rows(nc.scalar, w2_rows, 0, w2_scales)
+        nc.sync.dma_start(idx2[:], offs2)
         load_rows(nc.scalar, xo_rows, 0, xo_scales)
-        load_rows(nc.scalar, w_rows, 0, w_scales)
-        load_rows(nc.scalar, w_rows, R, w2_scales)
-        load_words(xt_all[:], xt_words)
-        load_words(w_raw[:], w_words)
-        load_words(w2_raw[:], w2_words)
-        load_words(xo_all[:], xo_words)
-        nc.sync.dma_start(idx3[:], offs3)
-
-        xt_picked_rows = tile("xt_picked_rows", J, U8)
-        xo_picked_rows = staging.tile([P, J], U8, name="xo_picked_rows", offset=2 * R, align_bytes=64)
-        planes1 = tile("planes1", 2 * J + 2 * R, U8)
-        nc.vector.tensor_copy(xt_picked_rows[:], xt_rows[:].indirect(idx[:]))
-        nc.vector.tensor_copy(xo_picked_rows[:], xo_rows[:].indirect(idx2[:]))
-        nc.gpsimd.tensor_copy(
-            planes1[:, 2 * J :].rearrange("p (i t m) -> p i t m", i=2, t=PACK),
-            w_rows[:].rearrange("p (i m t) -> p i t m", i=2, t=PACK),
-        )
-        nc.vector.tensor_copy(planes1[:, 0:J].bitcast(I32), xt_picked_rows[:].bitcast(I32))
-        nc.vector.tensor_copy(planes1[:, J : 2 * J].bitcast(I32), xo_picked_rows[:].bitcast(I32))
-        deal_rows(planes1)
-
-        planes2 = staging.tile([P, 2 * N + J], U8, name="planes2", offset=2 * R + J // 2 - (2 * N + J), align_bytes=64)
-        nc.gpsimd.memset(planes2[:].bitcast(I32), 0)
+        load_words(nc.sync, xt_all[:], xt_words)
+        early_planes = tile("early_planes", J + R, U8)
+        late_planes = tile("late_planes", J + R + 2 * N + J, U8)
+        planes2 = late_planes[:, J + R :]
         load_rows(nc.sync, planes2, 0, wb_scales)
+        nc.sync.dma_start(idx3[:], offs3)
+        load_words(nc.sync, w_raw[:], w_words)
         load_rows(nc.sync, planes2, N, ws_scales)
         load_rows(nc.sync, planes2, 2 * N, sx_scales)
+        load_words(nc.sync, w2_raw[:], w2_words)
+        load_words(nc.sync, xo_all[:], xo_words)
 
-        xt = staging.tile([P, J], U32, name="xt", offset=2 * R + J // 2, align_bytes=64)
+        pages = [tile("page%d" % n, E, F32) for n in range(2)]
+        for page in pages:
+            nc.vector.memset(page[:], 0.0)
+
+        def first_stage_planes(name, planes, table_rows, places, weight_rows):
+            picked = tile(name + "_picked", J, U8, tag="picked")
+            nc.vector.tensor_copy(picked[:], table_rows[:].indirect(places[:]))
+            nc.vector.tensor_copy(planes[:, 0:J].bitcast(I32), picked[:].bitcast(I32))
+            nc.gpsimd.tensor_copy(
+                planes[:, J : J + R].rearrange("p (t m) -> p t m", t=PACK), weight_rows[:].rearrange("p (m t) -> p t m", t=PACK)
+            )
+            deal_rows(nc.sync, planes)
+            return planes[:, 0:J], planes[:, J : J + R]
+
+        xt_plane, w_plane = first_stage_planes("xt", early_planes, xt_rows, idx, w_rows)
+        xo_plane, w2_plane = first_stage_planes("xo", late_planes, xo_rows, idx2, w2_rows)
+
+        xt = tile("xt", J, U32, tag="picked")
         xo = tile("xo", J, U16)
         nc.vector.tensor_copy(xt[:], xt_all[:].indirect(idx[:]))
         nc.vector.tensor_copy(xo[:], xo_all[:].indirect(idx2[:]))
 
-        second = sb.tile([P, 8 * N + 2 * J], U8, name="second", tag="table", align_bytes=64)
-        wb = second[:, 0 : 4 * N].bitcast(U32)
-        ws = second[:, 4 * N : 8 * N].bitcast(U32)
-        sx = second[:, 8 * N :].bitcast(U16)
-        load_words(ws, ws_words)
-        load_words(sx, sx_words)
-        load_words(wb, wb_words)
-        deal_rows(planes2)
-        pages = [shared.tile([P, E], F32, name="page%d" % n, offset=4 * E * n) for n in range(2)]
-        for page in pages:
-            nc.vector.memset(page[:], 0.0)
-
         w = tile("w", R, U32)
         w2 = tile("w2", R, U32)
         for dst, raw in ((w, w_raw), (w2, w2_raw)):
-            nc.scalar.copy(dst[:].rearrange("p (t m) -> p m t", t=PACK), raw[:].rearrange("p (m t) -> p m t", t=PACK))
+            nc.scalar.copy(
+                dst[:].rearrange("p (t g i) -> p g t i", t=PACK, i=4), raw[:].rearrange("p (g i t) -> p g t i", t=PACK, i=4)
+            )
 
-        w_plane, w2_plane = 2 * J, 2 * J + R
+        second = tile("second", 8 * N + 2 * J, U8, tag="table")
+        wb = second[:, 0 : 4 * N].bitcast(U32)
+        ws = second[:, 4 * N : 8 * N].bitcast(U32)
+        sx = second[:, 8 * N : 8 * N + 2 * J].bitcast(U16)
+        load_words(nc.sync, ws, ws_words)
+        load_words(nc.sync, sx, sx_words)
+        load_words(nc.sync, wb, wb_words)
 
         def passes(bank, h, weight, weight_plane, picked, picked_dtype, picked_plane, first):
-            j0 = h * HALF
+            js = slice(h * HALF, (h + 1) * HALF)
             for t in range(PACK):
                 cols = slice(t * P, (t + 1) * P)
                 nc.tensor.matmul_mx(
                     out=bank[:, cols],
                     lhsT=weight[:, cols].bitcast(E5M2),
-                    lhsT_scale=planes1[:, weight_plane + t * P : weight_plane + (t + 1) * P],
-                    rhs=picked[:, j0 : j0 + HALF].bitcast(picked_dtype),
-                    rhs_scale=planes1[:, picked_plane + j0 : picked_plane + j0 + HALF],
+                    lhsT_scale=weight_plane[:, cols],
+                    rhs=picked[:, js].bitcast(picked_dtype),
+                    rhs_scale=picked_plane[:, js],
                     start=first and t == 0, stop=(not first) and t == PACK - 1,
                 )
 
+        a_banks = [psum.tile([P, PACK * HALF], F32, name="a%d" % h) for h in range(2)]
+        b_banks = [psum.tile([P, PACK * HALF], F32, name="b%d" % h) for h in range(2)]
+        for h in range(2):
+            passes(a_banks[h], h, w, w_plane, xt, E4M3, xt_plane, True)
+
         hid_codes, hid_planes = [], []
         for h in range(2):
-            a_bank = psum.tile([P, PACK * HALF], F32, name="a%d" % h)
-            b_bank = psum.tile([P, PACK * HALF], F32, name="b%d" % h)
-            steps = [
-                (a_bank, h, w, w_plane, xt, E4M3, 0, True),
-                (b_bank, h, w2, w2_plane, xt, E4M3, 0, True),
-                (a_bank, h, w2, w2_plane, xo, E2M1, J, False),
-                (b_bank, h, w, w_plane, xo, E2M1, J, False),
-            ]
-            for i in ((0, 1, 2, 3) if h == 0 else (0, 2, 1, 3)):
-                passes(*steps[i])
+            a_bank, b_bank = a_banks[h], b_banks[h]
+            passes(a_bank, h, w2, w2_plane, xo, E2M1, xo_plane, False)
+            passes(b_bank, h, w2, w2_plane, xt, E4M3, xt_plane, True)
+            passes(b_bank, h, w, w_plane, xo, E2M1, xo_plane, False)
             a_sb = tile("a_sb%d" % h, PACK * HALF, F32)
             nc.scalar.copy(
                 a_sb[:].rearrange("p (j t) -> p j t", t=PACK), a_bank[:].rearrange("p (t j) -> p j t", t=PACK)
             )
-            hid = tile("hid%d" % h, PACK * HALF, BF16)
+            hid = tile("hid%d" % h, PACK * HALF, BF16, tag="hid")
             codes = tile("hid_codes%d" % h, HALF, U32)
             plane = tile("hid_plane%d" % h, HALF, U8)
             quarters = [slice(0, HALF // 2), slice(HALF // 2, HALF)]
@@ -173,32 +166,33 @@ def tile_list_crossed_direct_skip_scattered_kernel(
         for h in range(2):
             j0 = h * HALF
             places = idx3[:, h * HALF // 16 : (h + 1) * HALF // 16]
+            p_banks = [psum.tile([P, HALF], F32, name="p%d%d" % (h, n)) for n in range(2)]
+            p_sb = [tile("p_sb%d%d" % (h, n), HALF, F32, tag="hid" if (h, n) == (0, 0) else None) for n in range(2)]
             for n in range(2):
-                cols = slice(n * P, (n + 1) * P)
-                p_bank = psum.tile([P, HALF], F32, name="p%d%d" % (h, n))
                 nc.tensor.matmul_mx(
-                    out=p_bank[:],
-                    lhsT=ws[:, cols].bitcast(E5M2),
+                    out=p_banks[n][:],
+                    lhsT=ws[:, n * P : (n + 1) * P].bitcast(E5M2),
                     lhsT_scale=planes2[:, N + n * P : N + (n + 1) * P],
                     rhs=sx[:, j0 : j0 + HALF].bitcast(E2M1),
                     rhs_scale=planes2[:, 2 * N + j0 : 2 * N + j0 + HALF],
                     start=True, stop=False,
                 )
+            for n in range(2):
                 nc.tensor.matmul_mx(
-                    out=p_bank[:],
-                    lhsT=wb[:, cols].bitcast(E5M2),
-                    lhsT_scale=planes2[:, cols],
+                    out=p_banks[n][:],
+                    lhsT=wb[:, n * P : (n + 1) * P].bitcast(E5M2),
+                    lhsT_scale=planes2[:, n * P : (n + 1) * P],
                     rhs=hid_codes[h][:].bitcast(E4M3),
                     rhs_scale=hid_planes[h][:],
                     start=False, stop=True,
                 )
-                p_sb = tile("p_sb%d%d" % (h, n), HALF, F32)
-                if (h, n) == (1, 0):
-                    nc.vector.tensor_copy(p_sb[:], p_bank[:])
-                    nc.vector.tensor_copy(pages[n][:].indirect(places), p_sb[:])
-                else:
-                    nc.scalar.copy(p_sb[:], p_bank[:])
-                    nc.scalar.activation(pages[n][:].indirect(places), p_sb[:], COPY)
+            if h == 0:
+                nc.vector.tensor_copy(p_sb[0][:], p_banks[0][:])
+            else:
+                nc.scalar.copy(p_sb[0][:], p_banks[0][:])
+            nc.scalar.copy(p_sb[1][:], p_banks[1][:])
+            nc.vector.tensor_copy(pages[0][:].indirect(places), p_sb[0][:])
+            nc.scalar.activation(pages[1][:].indirect(places), p_sb[1][:], COPY)
 
-        for n in range(2):
-            nc.sync.dma_start(out=out[n * P : (n + 1) * P, :], in_=pages[n][:])
+        for n, queue in enumerate((nc.sync, nc.scalar)):
+            queue.dma_start(out=out[n * P : (n + 1) * P, :], in_=pages[n][:])

from contextlib import ExitStack

import concourse.mybir as mybir

K, T, Z, J, R, N, L, E = 512, 1024, 1024, 256, 512, 256, 512, 1024
FLOPS = 2 * J * (4 * K * R + R * N + L * N)

F32 = mybir.dt.float32
BF16 = mybir.dt.bfloat16
I32 = mybir.dt.int32
U32 = mybir.dt.uint32
U16 = mybir.dt.uint16
U8 = mybir.dt.uint8
E4M3 = mybir.dt.float8_e4m3fn_x4
E5M2 = mybir.dt.float8_e5m2_x4
E2M1 = mybir.dt.float4_e2m1fn_x4
MAX = mybir.AluOpType.max
COPY = mybir.ActivationFunctionType.Copy

P = 128
PACK = 4
ROWS = 16
HALF = 128


def tile_list_crossed_direct_skip_scattered_kernel(
    tc, xt_words, xt_scales, xo_words, xo_scales, w_words, w_scales, w2_words, w2_scales,
    wb_words, wb_scales, sx_words, sx_scales, ws_words, ws_scales, offs, offs2, offs3, out,
):
    nc = tc.nc
    with ExitStack() as ctx:
        lists = ctx.enter_context(tc.tile_pool(name="lists", bufs=1))
        sb = ctx.enter_context(tc.tile_pool(name="sb", bufs=1))
        psum = ctx.enter_context(tc.psum_pool(name="psum", bufs=1))

        def tile(name, width, dtype, tag=None):
            return sb.tile([P, width], dtype, name=name, tag=tag or name, align_bytes=64)

        def load_words(queue, dst, words):
            flat = words[0] if words.ndim == 3 else words[0].rearrange("p c t -> p (c t)")
            queue.dma_start(out=dst.bitcast(I32), in_=flat.bitcast(I32))

        def load_rows(queue, dst, col, scales):
            width = scales.shape[2]
            rows = scales[0].bitcast(I32).unsqueeze(1).to_broadcast([ROWS, P // ROWS, width // 4])
            queue.dma_start(out=dst[:, col : col + width].bitcast(I32), in_=rows)

        def deal_rows(queue, rows):
            for r in range(1, 4):
                queue.dma_start(out=rows[r:P:32, :].bitcast(I32), in_=rows[8 * r : P : 32, :].bitcast(I32))

        idx = lists.tile([P, J // 16], U16, name="idx")
        idx2 = lists.tile([P, J // 16], U16, name="idx2")
        idx3 = lists.tile([P, J // 16], U16, name="idx3")

        xt_rows = tile("xt_rows", T, U8)
        xo_rows = tile("xo_rows", Z, U8)
        xo_all = tile("xo_all", Z, U16)
        w_rows = tile("w_rows", R, U8)
        w2_rows = tile("w2_rows", R, U8)
        xt_all = tile("xt_all", T, U32, tag="table")
        w_raw = tile("w_raw", R, U32)
        w2_raw = tile("w2_raw", R, U32)

        nc.sync.dma_start(idx[:], offs)
        load_rows(nc.scalar, xt_rows, 0, xt_scales)
        load_rows(nc.sync, w_rows, 0, w_scales)
        load_rows(nc.scalar, w2_rows, 0, w2_scales)
        nc.sync.dma_start(idx2[:], offs2)
        load_rows(nc.scalar, xo_rows, 0, xo_scales)
        load_words(nc.sync, xt_all[:], xt_words)
        early_planes = tile("early_planes", J + R, U8)
        late_planes = tile("late_planes", J + R + 2 * N + J, U8)
        planes2 = late_planes[:, J + R :]
        load_rows(nc.sync, planes2, 0, wb_scales)
        nc.sync.dma_start(idx3[:], offs3)
        load_words(nc.sync, w_raw[:], w_words)
        load_rows(nc.sync, planes2, N, ws_scales)
        load_rows(nc.sync, planes2, 2 * N, sx_scales)
        load_words(nc.sync, w2_raw[:], w2_words)
        load_words(nc.sync, xo_all[:], xo_words)

        pages = [tile("page%d" % n, E, F32) for n in range(2)]
        for page in pages:
            nc.vector.memset(page[:], 0.0)

        def first_stage_planes(name, planes, table_rows, places, weight_rows):
            picked = tile(name + "_picked", J, U8, tag="picked")
            nc.vector.tensor_copy(picked[:], table_rows[:].indirect(places[:]))
            nc.vector.tensor_copy(planes[:, 0:J].bitcast(I32), picked[:].bitcast(I32))
            nc.gpsimd.tensor_copy(
                planes[:, J : J + R].rearrange("p (t m) -> p t m", t=PACK), weight_rows[:].rearrange("p (m t) -> p t m", t=PACK)
            )
            deal_rows(nc.sync, planes)
            return planes[:, 0:J], planes[:, J : J + R]

        xt_plane, w_plane = first_stage_planes("xt", early_planes, xt_rows, idx, w_rows)
        xo_plane, w2_plane = first_stage_planes("xo", late_planes, xo_rows, idx2, w2_rows)

        xt = tile("xt", J, U32, tag="picked")
        xo = tile("xo", J, U16)
        nc.vector.tensor_copy(xt[:], xt_all[:].indirect(idx[:]))
        nc.vector.tensor_copy(xo[:], xo_all[:].indirect(idx2[:]))

        w = tile("w", R, U32)
        w2 = tile("w2", R, U32)
        for dst, raw in ((w, w_raw), (w2, w2_raw)):
            nc.scalar.copy(
                dst[:].rearrange("p (t g i) -> p g t i", t=PACK, i=4), raw[:].rearrange("p (g i t) -> p g t i", t=PACK, i=4)
            )

        second = tile("second", 8 * N + 2 * J, U8, tag="table")
        wb = second[:, 0 : 4 * N].bitcast(U32)
        ws = second[:, 4 * N : 8 * N].bitcast(U32)
        sx = second[:, 8 * N : 8 * N + 2 * J].bitcast(U16)
        load_words(nc.sync, ws, ws_words)
        load_words(nc.sync, sx, sx_words)
        load_words(nc.sync, wb, wb_words)

        def passes(bank, h, weight, weight_plane, picked, picked_dtype, picked_plane, first):
            js = slice(h * HALF, (h + 1) * HALF)
            for t in range(PACK):
                cols = slice(t * P, (t + 1) * P)
                nc.tensor.matmul_mx(
                    out=bank[:, cols],
                    lhsT=weight[:, cols].bitcast(E5M2),
                    lhsT_scale=weight_plane[:, cols],
                    rhs=picked[:, js].bitcast(picked_dtype),
                    rhs_scale=picked_plane[:, js],
                    start=first and t == 0, stop=(not first) and t == PACK - 1,
                )

        a_banks = [psum.tile([P, PACK * HALF], F32, name="a%d" % h) for h in range(2)]
        b_banks = [psum.tile([P, PACK * HALF], F32, name="b%d" % h) for h in range(2)]
        for h in range(2):
            passes(a_banks[h], h, w, w_plane, xt, E4M3, xt_plane, True)

        hid_codes, hid_planes = [], []
        for h in range(2):
            a_bank, b_bank = a_banks[h], b_banks[h]
            passes(a_bank, h, w2, w2_plane, xo, E2M1, xo_plane, False)
            passes(b_bank, h, w2, w2_plane, xt, E4M3, xt_plane, True)
            passes(b_bank, h, w, w_plane, xo, E2M1, xo_plane, False)
            a_sb = tile("a_sb%d" % h, PACK * HALF, F32)
            nc.scalar.copy(
                a_sb[:].rearrange("p (j t) -> p j t", t=PACK), a_bank[:].rearrange("p (t j) -> p j t", t=PACK)
            )
            hid = tile("hid%d" % h, PACK * HALF, BF16, tag="hid")
            codes = tile("hid_codes%d" % h, HALF, U32)
            plane = tile("hid_plane%d" % h, HALF, U8)
            quarters = [slice(0, HALF // 2), slice(HALF // 2, HALF)]
            for js in quarters:
                nc.vector.tensor_tensor(
                    hid[:].rearrange("p (j t) -> p j t", t=PACK)[:, js, :],
                    a_sb[:].rearrange("p (j t) -> p j t", t=PACK)[:, js, :],
                    b_bank[:].rearrange("p (t j) -> p j t", t=PACK)[:, js, :],
                    MAX,
                )
            for js in quarters:
                nc.vector.quantize_mx(
                    out=codes[:, js].bitcast(E4M3), scales=plane[:, js], in_=hid[:, PACK * js.start : PACK * js.stop]
                )
            hid_codes.append(codes)
            hid_planes.append(plane)

        for h in range(2):
            j0 = h * HALF
            places = idx3[:, h * HALF // 16 : (h + 1) * HALF // 16]
            p_banks = [psum.tile([P, HALF], F32, name="p%d%d" % (h, n)) for n in range(2)]
            p_sb = [tile("p_sb%d%d" % (h, n), HALF, F32, tag="hid" if (h, n) == (0, 0) else None) for n in range(2)]
            for n in range(2):
                nc.tensor.matmul_mx(
                    out=p_banks[n][:],
                    lhsT=ws[:, n * P : (n + 1) * P].bitcast(E5M2),
                    lhsT_scale=planes2[:, N + n * P : N + (n + 1) * P],
                    rhs=sx[:, j0 : j0 + HALF].bitcast(E2M1),
                    rhs_scale=planes2[:, 2 * N + j0 : 2 * N + j0 + HALF],
                    start=True, stop=False,
                )
            for n in range(2):
                nc.tensor.matmul_mx(
                    out=p_banks[n][:],
                    lhsT=wb[:, n * P : (n + 1) * P].bitcast(E5M2),
                    lhsT_scale=planes2[:, n * P : (n + 1) * P],
                    rhs=hid_codes[h][:].bitcast(E4M3),
                    rhs_scale=hid_planes[h][:],
                    start=False, stop=True,
                )
            if h == 0:
                nc.vector.tensor_copy(p_sb[0][:], p_banks[0][:])
            else:
                nc.scalar.copy(p_sb[0][:], p_banks[0][:])
            nc.scalar.copy(p_sb[1][:], p_banks[1][:])
            nc.vector.tensor_copy(pages[0][:].indirect(places), p_sb[0][:])
            nc.scalar.activation(pages[1][:].indirect(places), p_sb[1][:], COPY)

        for n, queue in enumerate((nc.sync, nc.scalar)):
            queue.dma_start(out=out[n * P : (n + 1) * P, :], in_=pages[n][:])
